import numpy as np
import ml_dtypes


def mxq(x, axis, fmt="e4m3"):
    dtype, down = {"e4m3": (ml_dtypes.float8_e4m3fn, 7), "e5m2": (ml_dtypes.float8_e5m2, 14)}[fmt]
    v = np.moveaxis(np.asarray(x, np.float32).astype(ml_dtypes.bfloat16).astype(np.float64), axis, -1)
    blocks = v.reshape(v.shape[:-1] + (-1, 32))
    amax = np.abs(blocks).max(-1, keepdims=True)
    byte = np.maximum(np.where(amax > 0, np.frexp(amax)[1] - 1 + 127, 0) - down, 1)
    scale = np.exp2(byte - 127.0)
    codes = (blocks / scale).astype(np.float32).astype(dtype).astype(np.float64)
    return np.moveaxis((codes * scale).reshape(v.shape), -1, axis)


WIDE = False


def mx_kscale(k):
    if not WIDE:
        return np.ones(k)
    levels = np.array([10, -10, 5, -5, 0])
    if k % 512:
        return np.exp2(np.random.permutation(np.resize(levels, k // 32))).repeat(32)
    a = np.empty((k // 512, 16))
    for p in range(k // 512):
        a[p, :8] = np.random.permutation(np.resize(levels, 8))
        for g in range(8):
            far = levels[np.abs(levels - a[p, g]) >= 10]
            a[p, g + 8] = far[np.random.randint(len(far))]
    return np.exp2(a.ravel()).repeat(32)


def f64(x):
    return np.asarray(x).astype(np.float64)


def striped(idx):
    return np.tile(idx.reshape(-1, 16).T, (8, 1)).astype(np.uint16)


def unstriped(offs):
    return offs[:16].T.reshape(-1).astype(np.int64)


def striped8(idx):
    return np.concatenate([x.reshape(-1, 16).T for x in idx]).astype(np.uint16)


def runs(offs, k):
    lists = np.stack([offs[16 * r : 16 * r + 16].T.reshape(-1) for r in range(8)]).astype(np.int64)
    return lists[np.arange(k) % 512 // 64]


def pack_weight(w):
    k, n = w.shape
    w = f64(np.asarray(w, np.float32).astype(ml_dtypes.bfloat16)).reshape(k // 32, 32, n)
    amax = np.abs(w).max(1)
    byte = np.clip(np.where(amax > 0, np.frexp(amax)[1] - 1 + 127 - 7, 1), 1, 254)
    scaled = (w * np.exp2(127.0 - byte)[:, None, :]).reshape(k, n).astype(np.float32)
    words = np.ascontiguousarray(scaled.reshape(k // 512, 128, 4, n).transpose(0, 1, 3, 2)).astype(ml_dtypes.float8_e4m3fn).view(np.uint8)
    return words, np.ascontiguousarray(byte.astype(np.uint8).reshape(k // 512, 16, n))


def unpack_weight(words, scales):
    g, p, n, _ = words.shape
    vals = np.ascontiguousarray(words).view(ml_dtypes.float8_e4m3fn).astype(np.float64) * np.repeat(np.exp2(scales.astype(np.float64) - 127.0), 8, axis=1)[..., None]
    return vals.transpose(0, 1, 3, 2).reshape(g * 512, n)

def planes(y):
    n, m = y.shape
    v = y.astype(np.float32).astype(ml_dtypes.bfloat16).astype(np.float64).reshape(n // 32, 32, m)
    top = np.abs(v).max(1)
    byte = np.clip(np.where(top > 0, np.frexp(top)[1] - 1 + 127 - 7, 1), 1, 254)
    codes = (v * np.exp2(127.0 - byte)[:, None, :]).reshape(n, m).astype(np.float32).astype(ml_dtypes.float8_e4m3fn).view(np.uint8)
    words = codes.reshape(n // 512, 128, 4, m).transpose(0, 1, 3, 2)
    return np.ascontiguousarray(words), np.ascontiguousarray(byte.astype(np.uint8).reshape(n // 512, 16, m))


K, T, S, G, H, W, C, U = 512, 1024, 512, 2048, 512, 256, 512, 1024


def setup_inputs():
    n = np.random.standard_normal
    s = mx_kscale(K)[:, None]
    packed_xT = pack_weight(n((K, T)) * s)
    packed_dT = pack_weight(n((K, G)) / s)
    perm = np.stack([np.random.permutation(S) for _ in range(8)])
    perm2 = np.random.permutation(U)
    return {
        "x_words": packed_xT[0],
        "x_scales": packed_xT[1],
        "d_words": packed_dT[0],
        "d_scales": packed_dT[1],
        "gs": (np.random.uniform(0.5, 1.5, (K, 1)) / s).astype(np.float32),
        "offs": striped(np.random.permutation(T)[:S]),
        "k1": striped8(np.random.randint(0, G, (8, H))),
        "hz": striped8(np.random.randint(0, T, (8, S))),
        "k2": striped8(np.random.randint(0, G, (8, H))),
        "hy": striped8(np.random.randint(0, T, (8, S))),
        "k3": striped8(np.random.randint(0, G, (8, H))),
        "n1": striped8(perm[:, :W]),
        "n2": striped8(perm[:, W:]),
        "cand": striped(np.random.permutation(T)[:C]),
        "n3": striped(perm2[:S]),
        "n4": striped(perm2[S:]),
        "n5": striped(np.random.permutation(S)),
    }


def reference(x_words, x_scales, d_words, d_scales, gs, offs, k1, hz, k2, hy, k3, n1, n2, cand, n3, n4, n5):
    x_cand = unpack_weight(x_words, x_scales)[:, unstriped(cand)]
    d_k1 = unpack_weight(d_words, d_scales)[np.arange(K)[:, None], runs(k1, K)]
    xq = unpack_weight(x_words, x_scales)[:, unstriped(offs)]
    d_k2 = unpack_weight(d_words, d_scales)[np.arange(K)[:, None], runs(k2, K)]
    x_hz = unpack_weight(x_words, x_scales)[np.arange(K)[:, None], runs(hz, K)]
    d_k3 = unpack_weight(d_words, d_scales)[np.arange(K)[:, None], runs(k3, K)]
    x_hy = unpack_weight(x_words, x_scales)[np.arange(K)[:, None], runs(hy, K)]
    h = 0.0625 * (d_k1.T @ xq + d_k2.T @ x_hz + d_k3.T @ x_hy)
    pa = h[np.arange(H)[:, None], runs(n1, H)]
    pb = h[np.arange(H)[:, None], runs(n2, H)]
    rb = np.maximum(pa, pb)
    ra = pa / (np.abs(pb) + 0.5)
    ua = np.zeros((H, S))
    ua[np.arange(H)[:, None], runs(n1, H)] = ra
    ub = ua.copy()
    ub[np.arange(H)[:, None], runs(n2, H)] = rb
    z = f64(gs) * ub
    s = 0.0625 * ((x_cand.T @ mxq(z, 0, "e4m3")))
    ds = np.zeros((C, S))
    ds[:, unstriped(n5)] = s
    up = np.maximum(s, ds)
    ph = np.zeros((C, U))
    ph[:, unstriped(n3)] = ds
    out = ph.copy()
    out[:, unstriped(n4)] = up
    return (out,) + planes(out)

@@ -1,0 +1,276 @@
+from contextlib import ExitStack
+
+import concourse.mybir as mybir
+
+F32 = mybir.dt.float32
+BF16 = mybir.dt.bfloat16
+I32 = mybir.dt.int32
+U32 = mybir.dt.uint32
+U16 = mybir.dt.uint16
+U8 = mybir.dt.uint8
+FP8X4 = mybir.dt.float8_e4m3fn_x4
+ACT = mybir.ActivationFunctionType
+ALU = mybir.AluOpType
+
+P = 128
+K, T, S, G, H, W, C, U = 512, 1024, 512, 2048, 512, 256, 512, 1024
+FLOPS = 4 * 2 * 512 * 512 * 512
+ORDER = (2, 0, 1, 3)
+
+
+def tile_picked_mthhzcratiopagsn_none_po_kernel(
+    tc, x_words, x_scales, d_words, d_scales, gs, offs, k1, hz, k2, hy, k3, n1, n2, cand, n3, n4, n5, out_0, out_1, out_2
+):
+    nc = tc.nc
+    with ExitStack() as ctx:
+        pool = ctx.enter_context(tc.tile_pool(name="sb", bufs=1))
+        psum = ctx.enter_context(tc.psum_pool(name="ps", bufs=1))
+
+        def sb(name, cols, dtype, tag=None):
+            return pool.tile([P, cols], dtype, name=name, tag=tag or name, align_bytes=64)
+
+        def load_list(name, src):
+            tile = pool.tile([P, src.shape[1]], U16, name=name + "_list")
+            nc.sync.dma_start(tile[:], src)
+            return tile
+
+        d_runs = sb("d_runs", G, U8)
+        x_runs = sb("x_runs", T, U8)
+        x_rows = sb("x_rows", T, U8)
+        placed = sb("placed", 5 * S, U8)
+        half = sb("half", 1, F32)
+        for tile in (d_runs, x_runs, x_rows, placed):
+            nc.vector.memset(tile[:].bitcast(I32), 0)
+        nc.vector.memset(half[:], 0.5)
+
+        for e in range(2):
+            nc.sync.dma_start(d_runs[e:P:16, :].bitcast(I32), d_scales[0, e:16:2, :].bitcast(I32))
+        k1_t, k2_t, k3_t = load_list("k1", k1), load_list("k2", k2), load_list("k3", k3)
+        for e in range(2):
+            nc.sync.dma_start(x_runs[e:P:16, :].bitcast(I32), x_scales[0, e:16:2, :].bitcast(I32))
+        hz_t, hy_t, offs_t = load_list("hz", hz), load_list("hy", hy), load_list("offs", offs)
+        d_tab = sb("d_tab", G, U32)
+        nc.sync.dma_start(d_tab[:].bitcast(I32), d_words[0].rearrange("p n t -> p (n t)").bitcast(I32))
+        x_tab = sb("x_tab", T, U32)
+        nc.sync.dma_start(x_tab[:].bitcast(I32), x_words[0].rearrange("p n t -> p (n t)").bitcast(I32))
+        for c in range(4):
+            nc.sync.dma_start(x_rows[c:P:32, :].bitcast(I32), x_scales[0, c:16:4, :].bitcast(I32))
+        cand_t = load_list("cand", cand)
+        n2_t, n1_t = load_list("n2", n2), load_list("n1", n1)
+        gs_t = sb("gs_cols", 4, F32)
+        nc.sync.dma_start(gs_t[:], gs.rearrange("(p t) o -> p (t o)", t=4))
+        n5_t, n3_t, n4_t = load_list("n5", n5), load_list("n3", n3), load_list("n4", n4)
+
+        def gather(dst, window, offsets):
+            nc.vector.tensor_copy(dst, window[:].indirect(offsets[:]))
+
+        picked = sb("picked", 5 * S, U8)
+        for g, (table, offsets) in enumerate(((d_runs, k1_t), (d_runs, k2_t), (d_runs, k3_t), (x_runs, hz_t), (x_runs, hy_t))):
+            gather(picked[:, g * S : (g + 1) * S], table, offsets)
+        for c in range(4):
+            first = 16 * (c // 2) + c % 2
+            nc.scalar.dma_start(placed[c:P:32, :].bitcast(I32), picked[first:P:32, :].bitcast(I32))
+        xq_s = sb("xq_s", S, U8)
+        gather(xq_s[:], x_rows, offs_t)
+
+        d_pick = sb("d_pick", 3 * H, U32)
+        for g, offsets in enumerate((k1_t, k2_t, k3_t)):
+            gather(d_pick[:, g * H : (g + 1) * H], d_tab, offsets)
+        x_pick = [sb("x_pick%d" % g, S, U32) for g in range(3)]
+        gather(x_pick[0][:], x_tab, offs_t)
+        d_deal = sb("d_deal", 3 * H, U32)
+        nc.vector.tensor_copy(
+            d_deal[:].rearrange("p (g t a b) -> p g a t b", g=3, t=4, b=4),
+            d_pick[:].rearrange("p (g a b t) -> p g a t b", g=3, t=4, b=4),
+        )
+        ds_deal = sb("ds_deal", 3 * H, U8)
+        nc.vector.tensor_copy(
+            ds_deal[:].rearrange("p (g t m) -> p g t m", g=3, t=4),
+            placed[:, 0 : 3 * H].rearrange("p (g m t) -> p g t m", g=3, t=4),
+        )
+        gather(x_pick[1][:], x_tab, hz_t)
+        gather(x_pick[2][:], x_tab, hy_t)
+        x_sc = [xq_s[:], placed[:, 3 * S : 4 * S], placed[:, 4 * S : 5 * S]]
+
+        c_words = sb("c_words", C, U32)
+        gather(c_words[:].rearrange("p (t m) -> p m t", t=4), x_tab, cand_t)
+        c_sc = sb("c_sc", C, U8)
+        gather(c_sc[:].rearrange("p (t m) -> p m t", t=4), x_rows, cand_t)
+
+        h_ps = {}
+        for t in ORDER:
+            h_ps[t] = psum.tile([P, S], F32, name="h_ps%d" % t, tag="h_ps%d" % t)
+            for g in range(3):
+                cols = slice(g * H + t * P, g * H + (t + 1) * P)
+                nc.tensor.matmul_mx(
+                    out=h_ps[t][:],
+                    lhsT=d_deal[:, cols].bitcast(FP8X4),
+                    lhsT_scale=ds_deal[:, cols],
+                    rhs=x_pick[g][:].bitcast(FP8X4),
+                    rhs_scale=x_sc[g],
+                    start=(g == 0),
+                    stop=(g == 2),
+                )
+
+        pa, pb, inv, rb, ub = {}, {}, {}, {}, {}
+
+        def fetch(t):
+            h = sb("h%d" % t, S, F32)
+            nc.scalar.activation(h[:], h_ps[t][:], ACT.Copy, scale=0.0625)
+            pb[t] = sb("pb%d" % t, W, F32)
+            nc.scalar.activation(pb[t][:], h[:].indirect(n2_t[:]), ACT.Copy)
+            pa[t] = sb("pa%d" % t, W, F32)
+            nc.scalar.activation(pa[t][:], h[:].indirect(n1_t[:]), ACT.Copy)
+
+        def invert(t):
+            size = sb("size%d" % t, W, F32, tag="ub%d" % ORDER[0] if t == ORDER[3] else None)
+            nc.scalar.activation(size[:], pb[t][:], ACT.Abs)
+            root = sb("root%d" % t, W, F32)
+            nc.scalar.activation(root[:], size[:], ACT.Abs_reciprocal_sqrt, bias=half[:])
+            inv[t] = sb("inv%d" % t, W, F32)
+            nc.scalar.activation(inv[t][:], root[:], ACT.Square)
+
+        def larger(t):
+            rb[t] = sb("rb%d" % t, W, F32)
+            nc.vector.tensor_tensor(rb[t][:], pa[t][:], pb[t][:], ALU.max)
+
+        def put_rb(t):
+            ub[t] = sb("ub%d" % t, S, F32)
+            nc.vector.tensor_copy(ub[t][:].indirect(n2_t[:]), rb[t][:])
+
+        def put_ra(t):
+            nc.vector.tensor_tensor(ub[t][:].indirect(n1_t[:]), pa[t][:], inv[t][:], ALU.mult)
+
+        HALF = S // 2
+        z_bf = [sb("z_bf%d" % i, 4 * HALF, BF16) for i in range(2)]
+
+        def z_plane(t, on_vector):
+            for i in range(2):
+                dst = z_bf[i][:].rearrange("p (j t) -> p j t", t=4)[:, :, t]
+                src = ub[t][:, i * HALF : (i + 1) * HALF]
+                if on_vector:
+                    nc.vector.tensor_scalar(dst, src, gs_t[:, t : t + 1], None, ALU.mult)
+                else:
+                    nc.scalar.activation(dst, src, ACT.Copy, scale=gs_t[:, t : t + 1])
+
+        a, b, c, d = ORDER
+        fetch(a)
+        fetch(b)
+        invert(a)
+        fetch(c)
+        invert(b)
+        fetch(d)
+        invert(c)
+        larger(a)
+        put_rb(a)
+        larger(b)
+        put_ra(a)
+        z_plane(a, False)
+        invert(d)
+        put_rb(b)
+        larger(c)
+        put_ra(b)
+        larger(d)
+        put_rb(c)
+        put_rb(d)
+        put_ra(c)
+        put_ra(d)
+        for t in ORDER[1:]:
+            z_plane(t, t == d)
+
+        z_words = sb("z_words", S, U32)
+        z_sc = sb("z_sc", S, U8)
+        for i in range(2):
+            cols = slice(i * HALF, (i + 1) * HALF)
+            nc.vector.quantize_mx(out=z_words[:, cols].bitcast(FP8X4), scales=z_sc[:, cols], in_=z_bf[i][:])
+
+        s, ds, up, page = {}, {}, {}, {}
+
+        def score(t, pieces):
+            s[t] = sb("s%d" % t, S, F32, tag="page%d" % ORDER[0] if t == ORDER[3] else None)
+            width = S // pieces
+            rows = slice(t * P, (t + 1) * P)
+            for i in range(pieces):
+                cols = slice(i * width, (i + 1) * width)
+                bank = psum.tile([P, width], F32, name="s_ps%d_%d" % (t, i), tag=("h_ps%d" % ORDER[0] if i == 1 else "s_ps%d" % t))
+                nc.tensor.matmul_mx(
+                    out=bank[:],
+                    lhsT=c_words[:, rows].bitcast(FP8X4),
+                    lhsT_scale=c_sc[:, rows],
+                    rhs=z_words[:, cols].bitcast(FP8X4),
+                    rhs_scale=z_sc[:, cols],
+                    start=True,
+                    stop=True,
+                )
+                nc.scalar.activation(s[t][:, cols], bank[:], ACT.Copy, scale=0.0625)
+
+        def send(t, pieces):
+            ds[t] = sb("ds%d" % t, 2 * S, F32)
+            width = S // pieces
+            for i in range(pieces):
+                nc.vector.tensor_copy(
+                    ds[t][:].indirect(n5_t[:, i * width // 16 : (i + 1) * width // 16]), s[t][:, i * width : (i + 1) * width]
+                )
+
+        def raise_(t):
+            up[t] = sb("up%d" % t, S, F32)
+            nc.vector.tensor_tensor(up[t][:], s[t][:], ds[t][:, 0:S], ALU.max)
+
+        def put_ds(t):
+            page[t] = sb("page%d" % t, U, F32)
+            nc.vector.tensor_copy(page[t][:].indirect(n3_t[:]), ds[t][:, 0:S])
+
+        def put_up(t):
+            nc.vector.tensor_copy(page[t][:].indirect(n4_t[:]), up[t][:])
+
+        Q = U // 4
+        o_bf = [sb("o_bf%d" % i, 4 * Q, BF16) for i in range(4)]
+        rows_out = out_0.rearrange("(p t) w -> p t w", t=4)
+
+        def hand_out(t, on_vector):
+            nc.sync.dma_start(rows_out[:, t, :], page[t][:])
+            for i in range(4):
+                dst = o_bf[i][:].rearrange("p (j t) -> p j t", t=4)[:, :, t]
+                src = page[t][:, i * Q : (i + 1) * Q]
+                if i < on_vector:
+                    nc.vector.tensor_copy(dst, src)
+                else:
+                    nc.scalar.copy(dst, src)
+
+        score(a, 2)
+        score(b, 1)
+        score(c, 1)
+        send(a, 2)
+        send(b, 1)
+        raise_(a)
+        put_ds(a)
+        raise_(b)
+        put_up(a)
+        hand_out(a, 0)
+        score(d, 1)
+        send(c, 1)
+        put_ds(b)
+        raise_(c)
+        put_up(b)
+        hand_out(b, 0)
+        send(d, 1)
+        put_ds(c)
+        raise_(d)
+        put_ds(d)
+        put_up(c)
+        hand_out(c, 0)
+        put_up(d)
+        hand_out(d, 2)
+
+        o_words = sb("o_words", U, U32)
+        o_sc = sb("o_sc", U, U8)
+        words_out = out_1[0].rearrange("p n t -> p (n t)").bitcast(I32)
+        for i in range(4):
+            cols = slice(i * Q, (i + 1) * Q)
+            nc.vector.quantize_mx(out=o_words[:, cols].bitcast(FP8X4), scales=o_sc[:, cols], in_=o_bf[i][:])
+            if i % 2 == 1:
+                both = slice((i - 1) * Q, (i + 1) * Q)
+                nc.sync.dma_start(words_out[:, both], o_words[:, both].bitcast(I32))
+        for q in range(4):
+            queue = nc.scalar if q % 2 else nc.sync
+            queue.dma_start(out_2[0, 4 * q : 4 * q + 4, :].bitcast(I32), o_sc[32 * q : 32 * q + 4, :].bitcast(I32))

@@ -15,7 +15,7 @@ ALU = mybir.AluOpType
 P = 128
 K, T, S, G, H, W, C, U = 512, 1024, 512, 2048, 512, 256, 512, 1024
 FLOPS = 4 * 2 * 512 * 512 * 512
-ORDER = (2, 0, 1, 3)
+ORDER = (0, 2, 3, 1)
 
 
 def tile_picked_mthhzcratiopagsn_none_po_kernel(
@@ -24,38 +24,39 @@ def tile_picked_mthhzcratiopagsn_none_po_kernel(
     nc = tc.nc
     with ExitStack() as ctx:
         pool = ctx.enter_context(tc.tile_pool(name="sb", bufs=1))
+        reused = ctx.enter_context(tc.tile_pool(name="reused", bufs=1))
         psum = ctx.enter_context(tc.psum_pool(name="ps", bufs=1))
 
         def sb(name, cols, dtype, tag=None):
             return pool.tile([P, cols], dtype, name=name, tag=tag or name, align_bytes=64)
+
+        def at(name, cols, dtype, offset):
+            return reused.tile([P, cols], dtype, name=name, align_bytes=64, offset=offset)
 
         def load_list(name, src):
             tile = pool.tile([P, src.shape[1]], U16, name=name + "_list")
             nc.sync.dma_start(tile[:], src)
             return tile
 
-        d_runs = sb("d_runs", G, U8)
+        d_runs = at("d_runs", G, U8, 15872)
         x_runs = sb("x_runs", T, U8)
-        x_rows = sb("x_rows", T, U8)
-        placed = sb("placed", 5 * S, U8)
+        placed = sb("placed", 7 * S, U8)
         half = sb("half", 1, F32)
-        for tile in (d_runs, x_runs, x_rows, placed):
-            nc.vector.memset(tile[:].bitcast(I32), 0)
+        nc.vector.memset(placed[:].bitcast(I32), 0)
         nc.vector.memset(half[:], 0.5)
 
-        for e in range(2):
-            nc.sync.dma_start(d_runs[e:P:16, :].bitcast(I32), d_scales[0, e:16:2, :].bitcast(I32))
+        def load_blocks(tile, rows):
+            nc.sync.dma_start(tile[:].bitcast(I32), rows.bitcast(I32).unsqueeze(1).to_broadcast([16, 8, rows.shape[1] // 4]))
+
+        load_blocks(x_runs, x_scales[0])
+        hz_t, hy_t = load_list("hz", hz), load_list("hy", hy)
+        offs_t, cand_t = load_list("offs", offs), load_list("cand", cand)
+        load_blocks(d_runs, d_scales[0])
         k1_t, k2_t, k3_t = load_list("k1", k1), load_list("k2", k2), load_list("k3", k3)
-        for e in range(2):
-            nc.sync.dma_start(x_runs[e:P:16, :].bitcast(I32), x_scales[0, e:16:2, :].bitcast(I32))
-        hz_t, hy_t, offs_t = load_list("hz", hz), load_list("hy", hy), load_list("offs", offs)
-        d_tab = sb("d_tab", G, U32)
+        d_tab = at("d_tab", G, U32, 7680)
         nc.sync.dma_start(d_tab[:].bitcast(I32), d_words[0].rearrange("p n t -> p (n t)").bitcast(I32))
         x_tab = sb("x_tab", T, U32)
         nc.sync.dma_start(x_tab[:].bitcast(I32), x_words[0].rearrange("p n t -> p (n t)").bitcast(I32))
-        for c in range(4):
-            nc.sync.dma_start(x_rows[c:P:32, :].bitcast(I32), x_scales[0, c:16:4, :].bitcast(I32))
-        cand_t = load_list("cand", cand)
         n2_t, n1_t = load_list("n2", n2), load_list("n1", n1)
         gs_t = sb("gs_cols", 4, F32)
         nc.sync.dma_start(gs_t[:], gs.rearrange("(p t) o -> p (t o)", t=4))
@@ -64,55 +65,63 @@ def tile_picked_mthhzcratiopagsn_none_po_kernel(
         def gather(dst, window, offsets):
             nc.vector.tensor_copy(dst, window[:].indirect(offsets[:]))
 
-        picked = sb("picked", 5 * S, U8)
-        for g, (table, offsets) in enumerate(((d_runs, k1_t), (d_runs, k2_t), (d_runs, k3_t), (x_runs, hz_t), (x_runs, hy_t))):
-            gather(picked[:, g * S : (g + 1) * S], table, offsets)
+        x_pick = [sb("x_pick%d" % g, S, U32) for g in range(2)]
+        picked = at("picked", 7 * S, U8, 4096)
+        for g, offsets in ((4, hz_t), (5, hy_t), (3, offs_t)):
+            gather(picked[:, g * S : (g + 1) * S], x_runs, offsets)
+        gather(picked[:, 6 * S : 7 * S].rearrange("p (t m) -> p m t", t=4), x_runs, cand_t)
+        for g, offsets in enumerate((k1_t, k2_t, k3_t)):
+            gather(picked[:, g * S : (g + 1) * S], d_runs, offsets)
         for c in range(4):
-            first = 16 * (c // 2) + c % 2
+            first = 8 * c
             nc.scalar.dma_start(placed[c:P:32, :].bitcast(I32), picked[first:P:32, :].bitcast(I32))
-        xq_s = sb("xq_s", S, U8)
-        gather(xq_s[:], x_rows, offs_t)
 
-        d_pick = sb("d_pick", 3 * H, U32)
+        d_pick = at("d_pick", 3 * H, U32, 15872)
         for g, offsets in enumerate((k1_t, k2_t, k3_t)):
             gather(d_pick[:, g * H : (g + 1) * H], d_tab, offsets)
-        x_pick = [sb("x_pick%d" % g, S, U32) for g in range(3)]
         gather(x_pick[0][:], x_tab, offs_t)
-        d_deal = sb("d_deal", 3 * H, U32)
-        nc.vector.tensor_copy(
-            d_deal[:].rearrange("p (g t a b) -> p g a t b", g=3, t=4, b=4),
-            d_pick[:].rearrange("p (g a b t) -> p g a t b", g=3, t=4, b=4),
-        )
-        ds_deal = sb("ds_deal", 3 * H, U8)
-        nc.vector.tensor_copy(
-            ds_deal[:].rearrange("p (g t m) -> p g t m", g=3, t=4),
-            placed[:, 0 : 3 * H].rearrange("p (g m t) -> p g t m", g=3, t=4),
-        )
         gather(x_pick[1][:], x_tab, hz_t)
+        G3 = 3 * P
+        d_first = sb("d_first", G3, U32)
+        nc.vector.tensor_copy(d_first[:], d_pick[:].rearrange("p (m t) -> p t m", t=4)[:, 0, :])
+        ds_first = at("ds_first", G3, U8, 9216)
+        nc.vector.tensor_copy(ds_first[:], placed[:, 0 : 3 * H].rearrange("p (m t) -> p t m", t=4)[:, 0, :])
+        x_pick.append(at("x_pick2", S, U32, 6656))
         gather(x_pick[2][:], x_tab, hy_t)
-        x_sc = [xq_s[:], placed[:, 3 * S : 4 * S], placed[:, 4 * S : 5 * S]]
+        d_rest = at("d_rest", 3 * G3, U32, 0)
+        nc.vector.tensor_copy(
+            d_rest[:].rearrange("p (t a b) -> p a t b", t=3, b=4),
+            d_pick[:].rearrange("p (a b t) -> p a t b", t=4, b=4)[:, :, 1:4, :],
+        )
+        ds_rest = at("ds_rest", 3 * G3, U8, 9600)
+        nc.vector.tensor_copy(
+            ds_rest[:].rearrange("p (t a b) -> p a t b", t=3, b=16),
+            placed[:, 0 : 3 * H].rearrange("p (a b t) -> p a t b", t=4, b=16)[:, :, 1:4, :],
+        )
+        x_sc = [placed[:, (3 + g) * S : (4 + g) * S] for g in range(3)]
 
-        c_words = sb("c_words", C, U32)
+        c_words = at("c_words", C, U32, 17024)
         gather(c_words[:].rearrange("p (t m) -> p m t", t=4), x_tab, cand_t)
-        c_sc = sb("c_sc", C, U8)
-        gather(c_sc[:].rearrange("p (t m) -> p m t", t=4), x_rows, cand_t)
+        c_sc = placed[:, 6 * S : 7 * S]
 
         h_ps = {}
         for t in ORDER:
             h_ps[t] = psum.tile([P, S], F32, name="h_ps%d" % t, tag="h_ps%d" % t)
             for g in range(3):
-                cols = slice(g * H + t * P, g * H + (t + 1) * P)
+                first = (3 * max(t - 1, 0) + g) * P
+                cols = slice(first, first + P)
+                words, scales = (d_first, ds_first) if t == 0 else (d_rest, ds_rest)
                 nc.tensor.matmul_mx(
                     out=h_ps[t][:],
-                    lhsT=d_deal[:, cols].bitcast(FP8X4),
-                    lhsT_scale=ds_deal[:, cols],
+                    lhsT=words[:, cols].bitcast(FP8X4),
+                    lhsT_scale=scales[:, cols],
                     rhs=x_pick[g][:].bitcast(FP8X4),
                     rhs_scale=x_sc[g],
                     start=(g == 0),
                     stop=(g == 2),
                 )
 
-        pa, pb, inv, rb, ub = {}, {}, {}, {}, {}
+        pa, pb, inv, rb, ub, roots = {}, {}, {}, {}, {}, {}
 
         def fetch(t):
             h = sb("h%d" % t, S, F32)
@@ -123,12 +132,15 @@ def tile_picked_mthhzcratiopagsn_none_po_kernel(
             nc.scalar.activation(pa[t][:], h[:].indirect(n1_t[:]), ACT.Copy)
 
         def invert(t):
-            size = sb("size%d" % t, W, F32, tag="ub%d" % ORDER[0] if t == ORDER[3] else None)
+            size = at("size%d" % t, W, F32, 22528 + 1536) if t == d else sb("size%d" % t, W, F32)
             nc.scalar.activation(size[:], pb[t][:], ACT.Abs)
             root = sb("root%d" % t, W, F32)
             nc.scalar.activation(root[:], size[:], ACT.Abs_reciprocal_sqrt, bias=half[:])
-            inv[t] = sb("inv%d" % t, W, F32)
-            nc.scalar.activation(inv[t][:], root[:], ACT.Square)
+            roots[t] = root
+
+        def square(t):
+            inv[t] = sb("inv%d" % t, W, F32, tag="ub%d" % a if t == d else None)
+            nc.scalar.activation(inv[t][:], roots[t][:], ACT.Square)
 
         def larger(t):
             rb[t] = sb("rb%d" % t, W, F32)
@@ -142,7 +154,7 @@ def tile_picked_mthhzcratiopagsn_none_po_kernel(
             nc.vector.tensor_tensor(ub[t][:].indirect(n1_t[:]), pa[t][:], inv[t][:], ALU.mult)
 
         HALF = S // 2
-        z_bf = [sb("z_bf%d" % i, 4 * HALF, BF16) for i in range(2)]
+        z_bf = []
 
         def z_plane(t, on_vector):
             for i in range(2):
@@ -157,16 +169,22 @@ def tile_picked_mthhzcratiopagsn_none_po_kernel(
         fetch(a)
         fetch(b)
         invert(a)
+        square(a)
         fetch(c)
         invert(b)
+        square(b)
         fetch(d)
         invert(c)
+        invert(d)
+        square(c)
+        z_bf.append(at("z_bf0", 4 * HALF, BF16, 22528))
+        z_bf.append(at("z_bf1", 4 * HALF, BF16, 22528 + 2048))
         larger(a)
         put_rb(a)
         larger(b)
         put_ra(a)
         z_plane(a, False)
-        invert(d)
+        square(d)
         put_rb(b)
         larger(c)
         put_ra(b)
@@ -184,15 +202,17 @@ def tile_picked_mthhzcratiopagsn_none_po_kernel(
             cols = slice(i * HALF, (i + 1) * HALF)
             nc.vector.quantize_mx(out=z_words[:, cols].bitcast(FP8X4), scales=z_sc[:, cols], in_=z_bf[i][:])
 
-        s, ds, up, page = {}, {}, {}, {}
+        s, s_ps, ds, up, page = {}, {}, {}, {}, {}
 
-        def score(t, pieces):
-            s[t] = sb("s%d" % t, S, F32, tag="page%d" % ORDER[0] if t == ORDER[3] else None)
+        def score(t, pieces, which):
+            if 0 in which:
+                s[t] = sb("s%d" % t, S, F32)
             width = S // pieces
             rows = slice(t * P, (t + 1) * P)
-            for i in range(pieces):
+            for i in which:
                 cols = slice(i * width, (i + 1) * width)
-                bank = psum.tile([P, width], F32, name="s_ps%d_%d" % (t, i), tag=("h_ps%d" % ORDER[0] if i == 1 else "s_ps%d" % t))
+                bank = psum.tile([P, width], F32, name="s_ps%d_%d" % (t, i), tag=("h_ps%d" % t if i == 1 else "s_ps%d" % (c if t == d else t)))
+                s_ps[t] = bank
                 nc.tensor.matmul_mx(
                     out=bank[:],
                     lhsT=c_words[:, rows].bitcast(FP8X4),
@@ -204,17 +224,21 @@ def tile_picked_mthhzcratiopagsn_none_po_kernel(
                 )
                 nc.scalar.activation(s[t][:, cols], bank[:], ACT.Copy, scale=0.0625)
 
-        def send(t, pieces):
-            ds[t] = sb("ds%d" % t, 2 * S, F32)
+        def send(t, pieces, which):
+            if 0 in which:
+                ds[t] = sb("ds%d" % t, 2 * S, F32)
             width = S // pieces
-            for i in range(pieces):
+            for i in which:
                 nc.vector.tensor_copy(
                     ds[t][:].indirect(n5_t[:, i * width // 16 : (i + 1) * width // 16]), s[t][:, i * width : (i + 1) * width]
                 )
 
         def raise_(t):
             up[t] = sb("up%d" % t, S, F32)
-            nc.vector.tensor_tensor(up[t][:], s[t][:], ds[t][:, 0:S], ALU.max)
+            if t == c:
+                nc.vector.scalar_tensor_tensor(up[t][:], s_ps[t][:], 0.0625, ds[t][:, 0:S], ALU.mult, ALU.max)
+            else:
+                nc.vector.tensor_tensor(up[t][:], s[t][:], ds[t][:, 0:S], ALU.max)
 
         def put_ds(t):
             page[t] = sb("page%d" % t, U, F32)
@@ -227,9 +251,10 @@ def tile_picked_mthhzcratiopagsn_none_po_kernel(
         o_bf = [sb("o_bf%d" % i, 4 * Q, BF16) for i in range(4)]
         rows_out = out_0.rearrange("(p t) w -> p t w", t=4)
 
-        def hand_out(t, on_vector):
-            nc.sync.dma_start(rows_out[:, t, :], page[t][:])
-            for i in range(4):
+        def hand_out(t, on_vector, chunks=range(4)):
+            if 0 in chunks:
+                nc.sync.dma_start(rows_out[:, t, :], page[t][:])
+            for i in chunks:
                 dst = o_bf[i][:].rearrange("p (j t) -> p j t", t=4)[:, :, t]
                 src = page[t][:, i * Q : (i + 1) * Q]
                 if i < on_vector:
@@ -237,28 +262,31 @@ def tile_picked_mthhzcratiopagsn_none_po_kernel(
                 else:
                     nc.scalar.copy(dst, src)
 
-        score(a, 2)
-        score(b, 1)
-        score(c, 1)
-        send(a, 2)
-        send(b, 1)
+        for i in range(2):
+            score(a, 2, [i])
+            score(b, 2, [i])
+        score(c, 1, [0])
+        for i in range(2):
+            send(a, 2, [i])
+            send(b, 2, [i])
         raise_(a)
         put_ds(a)
-        raise_(b)
+        send(c, 1, [0])
         put_up(a)
-        hand_out(a, 0)
-        score(d, 1)
-        send(c, 1)
-        put_ds(b)
+        hand_out(a, 0, range(2))
         raise_(c)
+        score(d, 1, [0])
+        hand_out(a, 0, range(2, 4))
+        put_ds(b)
+        raise_(b)
+        put_ds(c)
         put_up(b)
         hand_out(b, 0)
-        send(d, 1)
-        put_ds(c)
-        raise_(d)
-        put_ds(d)
+        send(d, 1, [0])
         put_up(c)
         hand_out(c, 0)
+        raise_(d)
+        put_ds(d)
         put_up(d)
         hand_out(d, 2)
 

@@ -44,6 +44,8 @@ def tile_picked_mthhzcratiopagsn_none_po_kernel(
         half = sb("half", 1, F32)
         nc.vector.memset(placed[:].bitcast(I32), 0)
         nc.vector.memset(half[:], 0.5)
+        warm = sb("warm", 1, F32)
+        nc.scalar.activation(warm[:], half[:], ACT.Abs_reciprocal_sqrt, bias=half[:])
 
         def load_blocks(tile, rows):
             nc.sync.dma_start(tile[:].bitcast(I32), rows.bitcast(I32).unsqueeze(1).to_broadcast([16, 8, rows.shape[1] // 4]))

@@ -13,9 +13,25 @@ ACT = mybir.ActivationFunctionType
 ALU = mybir.AluOpType
 
 P = 128
-K, T, S, G, H, W, C, U = 512, 1024, 512, 2048, 512, 256, 512, 1024
-FLOPS = 4 * 2 * 512 * 512 * 512
-ORDER = (0, 2, 3, 1)
+PACK = 4
+GROUP = 16
+TOKENS, CODEWORDS = 1024, 2048
+N = 512
+PAIRS = 256
+SLOTS = 1024
+TERMS = 3
+SIXTEENTH = 0.0625
+FLOPS = 4 * 2 * N * N * N
+
+A, B, C, D = 0, 2, 3, 1
+
+Z_PARTS = (slice(0, 128), slice(128, 256), slice(256, 512))
+O_PARTS = tuple(slice(256 * i, 256 * (i + 1)) for i in range(4))
+VECTOR_PARTS = 2
+
+
+def width(cols):
+    return cols.stop - cols.start
 
 
 def tile_picked_mthhzcratiopagsn_none_po_kernel(
@@ -27,280 +43,275 @@ def tile_picked_mthhzcratiopagsn_none_po_kernel(
         reused = ctx.enter_context(tc.tile_pool(name="reused", bufs=1))
         psum = ctx.enter_context(tc.psum_pool(name="ps", bufs=1))
 
-        def sb(name, cols, dtype, tag=None):
-            return pool.tile([P, cols], dtype, name=name, tag=tag or name, align_bytes=64)
+        def sb(name, cols, dtype, after=None):
+            return pool.tile([P, cols], dtype, name=name, tag=after or name, align_bytes=64)
 
         def at(name, cols, dtype, offset):
             return reused.tile([P, cols], dtype, name=name, align_bytes=64, offset=offset)
+
+        at_d_rest = 0
+        at_picked = 4096
+        at_d_tab = at_picked + 2 * TERMS * N
+        at_x_last = at_d_tab - 1024
+        at_ds_first = at_x_last + 4 * N
+        at_ds_rest = at_ds_first + TERMS * P
+        at_d_pick = at_d_tab + 4 * CODEWORDS
+        at_z = at_d_pick + 4 * TERMS * N
 
         def load_list(name, src):
             tile = pool.tile([P, src.shape[1]], U16, name=name + "_list")
             nc.sync.dma_start(tile[:], src)
             return tile
 
-        d_runs = at("d_runs", G, U8, 15872)
-        x_runs = sb("x_runs", T, U8)
-        placed = sb("placed", 7 * S, U8)
-        half = sb("half", 1, F32)
-        nc.vector.memset(placed[:].bitcast(I32), 0)
-        nc.vector.memset(half[:], 0.5)
-        warm = sb("warm", 1, F32)
-        nc.scalar.activation(warm[:], half[:], ACT.Abs_reciprocal_sqrt, bias=half[:])
-
         def load_blocks(tile, rows):
             nc.sync.dma_start(tile[:].bitcast(I32), rows.bitcast(I32).unsqueeze(1).to_broadcast([16, 8, rows.shape[1] // 4]))
 
-        load_blocks(x_runs, x_scales[0])
-        hz_t, hy_t = load_list("hz", hz), load_list("hy", hy)
-        offs_t, cand_t = load_list("offs", offs), load_list("cand", cand)
-        load_blocks(d_runs, d_scales[0])
-        k1_t, k2_t, k3_t = load_list("k1", k1), load_list("k2", k2), load_list("k3", k3)
-        d_tab = at("d_tab", G, U32, 7680)
-        nc.sync.dma_start(d_tab[:].bitcast(I32), d_words[0].rearrange("p n t -> p (n t)").bitcast(I32))
-        x_tab = sb("x_tab", T, U32)
-        nc.sync.dma_start(x_tab[:].bitcast(I32), x_words[0].rearrange("p n t -> p (n t)").bitcast(I32))
-        n2_t, n1_t = load_list("n2", n2), load_list("n1", n1)
-        gs_t = sb("gs_cols", 4, F32)
-        nc.sync.dma_start(gs_t[:], gs.rearrange("(p t) o -> p (t o)", t=4))
-        n5_t, n3_t, n4_t = load_list("n5", n5), load_list("n3", n3), load_list("n4", n4)
+        def load_words(tile, words):
+            nc.sync.dma_start(tile[:].bitcast(I32), words.rearrange("p n t -> p (n t)").bitcast(I32))
 
         def gather(dst, window, offsets):
             nc.vector.tensor_copy(dst, window[:].indirect(offsets[:]))
 
-        x_pick = [sb("x_pick%d" % g, S, U32) for g in range(2)]
-        picked = at("picked", 7 * S, U8, 4096)
-        for g, offsets in ((4, hz_t), (5, hy_t), (3, offs_t)):
-            gather(picked[:, g * S : (g + 1) * S], x_runs, offsets)
-        gather(picked[:, 6 * S : 7 * S].rearrange("p (t m) -> p m t", t=4), x_runs, cand_t)
-        for g, offsets in enumerate((k1_t, k2_t, k3_t)):
-            gather(picked[:, g * S : (g + 1) * S], d_runs, offsets)
-        for c in range(4):
-            first = 8 * c
-            nc.scalar.dma_start(placed[c:P:32, :].bitcast(I32), picked[first:P:32, :].bitcast(I32))
+        def place(queue, dst, src):
+            for c in range(4):
+                queue.dma_start(dst[c:P:32, :].bitcast(I32), src[8 * c : P : 32, :].bitcast(I32))
 
-        d_pick = at("d_pick", 3 * H, U32, 15872)
-        for g, offsets in enumerate((k1_t, k2_t, k3_t)):
-            gather(d_pick[:, g * H : (g + 1) * H], d_tab, offsets)
+        def dealt(ap):
+            return ap.rearrange("p (t m) -> p m t", t=PACK)
+
+        placed = sb("placed", 2 * TERMS * N, U8)
+        c_scales = sb("c_scales", N, U8)
+        for tile in (placed, c_scales):
+            nc.vector.memset(tile[:].bitcast(I32), 0)
+        half = sb("half", 1, F32)
+        nc.vector.memset(half[:], 0.5)
+        warm = sb("warm", 1, F32)
+        nc.scalar.activation(warm[:], half[:], ACT.Abs_reciprocal_sqrt, bias=half[:])
+
+        x_blocks = sb("x_blocks", TOKENS, U8)
+        load_blocks(x_blocks, x_scales[0])
+        hz_t, hy_t, offs_t = load_list("hz", hz), load_list("hy", hy), load_list("offs", offs)
+        d_blocks = at("d_blocks", CODEWORDS, U8, at_d_pick)
+        load_blocks(d_blocks, d_scales[0])
+        k_t = [load_list("k1", k1), load_list("k2", k2), load_list("k3", k3)]
+        d_tab = at("d_tab", CODEWORDS, U32, at_d_tab)
+        load_words(d_tab, d_words[0])
+        x_tab = sb("x_tab", TOKENS, U32)
+        load_words(x_tab, x_words[0])
+        cand_t, n2_t, n1_t = load_list("cand", cand), load_list("n2", n2), load_list("n1", n1)
+        gs_t = sb("gs_cols", PACK, F32)
+        nc.sync.dma_start(gs_t[:], gs.rearrange("(p t) o -> p (t o)", t=PACK))
+        n5_t, n3_t, n4_t = load_list("n5", n5), load_list("n3", n3), load_list("n4", n4)
+
+        picked = at("picked", 2 * TERMS * N, U8, at_picked)
+        for g, offsets in ((4, hz_t), (5, hy_t), (3, offs_t)):
+            gather(picked[:, g * N : (g + 1) * N], x_blocks, offsets)
+        for g in range(TERMS):
+            gather(picked[:, g * N : (g + 1) * N], d_blocks, k_t[g])
+        place(nc.scalar, placed, picked)
+
+        d_pick = at("d_pick", TERMS * N, U32, at_d_pick)
+        for g in range(TERMS):
+            gather(d_pick[:, g * N : (g + 1) * N], d_tab, k_t[g])
+        x_pick = [sb("x_offs", N, U32), sb("x_hz", N, U32)]
         gather(x_pick[0][:], x_tab, offs_t)
         gather(x_pick[1][:], x_tab, hz_t)
-        G3 = 3 * P
-        d_first = sb("d_first", G3, U32)
-        nc.vector.tensor_copy(d_first[:], d_pick[:].rearrange("p (m t) -> p t m", t=4)[:, 0, :])
-        ds_first = at("ds_first", G3, U8, 9216)
-        nc.vector.tensor_copy(ds_first[:], placed[:, 0 : 3 * H].rearrange("p (m t) -> p t m", t=4)[:, 0, :])
-        x_pick.append(at("x_pick2", S, U32, 6656))
+        d_scale_bytes = placed[:, 0 : TERMS * N]
+        d_first = sb("d_first", TERMS * P, U32)
+        nc.vector.tensor_copy(d_first[:], d_pick[:].rearrange("p (m t) -> p t m", t=PACK)[:, 0, :])
+        ds_first = at("ds_first", TERMS * P, U8, at_ds_first)
+        nc.vector.tensor_copy(ds_first[:], d_scale_bytes.rearrange("p (m t) -> p t m", t=PACK)[:, 0, :])
+        x_pick.append(at("x_last", N, U32, at_x_last))
         gather(x_pick[2][:], x_tab, hy_t)
-        d_rest = at("d_rest", 3 * G3, U32, 0)
+        d_rest = at("d_rest", (PACK - 1) * TERMS * P, U32, at_d_rest)
         nc.vector.tensor_copy(
-            d_rest[:].rearrange("p (t a b) -> p a t b", t=3, b=4),
-            d_pick[:].rearrange("p (a b t) -> p a t b", t=4, b=4)[:, :, 1:4, :],
+            d_rest[:].rearrange("p (t a b) -> p a t b", t=PACK - 1, b=4),
+            d_pick[:].rearrange("p (a b t) -> p a t b", t=PACK, b=4)[:, :, 1:PACK, :],
         )
-        ds_rest = at("ds_rest", 3 * G3, U8, 9600)
+        ds_rest = at("ds_rest", (PACK - 1) * TERMS * P, U8, at_ds_rest)
         nc.vector.tensor_copy(
-            ds_rest[:].rearrange("p (t a b) -> p a t b", t=3, b=16),
-            placed[:, 0 : 3 * H].rearrange("p (a b t) -> p a t b", t=4, b=16)[:, :, 1:4, :],
+            ds_rest[:].rearrange("p (t a b) -> p a t b", t=PACK - 1, b=16),
+            d_scale_bytes.rearrange("p (a b t) -> p a t b", t=PACK, b=16)[:, :, 1:PACK, :],
         )
-        x_sc = [placed[:, (3 + g) * S : (4 + g) * S] for g in range(3)]
 
-        c_words = at("c_words", C, U32, 17024)
-        gather(c_words[:].rearrange("p (t m) -> p m t", t=4), x_tab, cand_t)
-        c_sc = placed[:, 6 * S : 7 * S]
+        c_words = at("c_words", N, U32, at_d_pick)
+        gather(dealt(c_words[:]), x_tab, cand_t)
+        c_picked = at("c_picked", N, U8, at_d_pick + 4 * N)
+        gather(dealt(c_picked[:]), x_blocks, cand_t)
+        place(nc.sync, c_scales, c_picked)
 
         h_ps = {}
-        for t in ORDER:
-            h_ps[t] = psum.tile([P, S], F32, name="h_ps%d" % t, tag="h_ps%d" % t)
-            for g in range(3):
-                first = (3 * max(t - 1, 0) + g) * P
-                cols = slice(first, first + P)
-                words, scales = (d_first, ds_first) if t == 0 else (d_rest, ds_rest)
+        for t in (A, B, C, D):
+            h_ps[t] = psum.tile([P, N], F32, name="h_ps%d" % t, tag="bank%d" % t)
+            words, scales = (d_first, ds_first) if t == 0 else (d_rest, ds_rest)
+            for g in range(TERMS):
+                first = (TERMS * max(t - 1, 0) + g) * P
                 nc.tensor.matmul_mx(
                     out=h_ps[t][:],
-                    lhsT=words[:, cols].bitcast(FP8X4),
-                    lhsT_scale=scales[:, cols],
+                    lhsT=words[:, first : first + P].bitcast(FP8X4),
+                    lhsT_scale=scales[:, first : first + P],
                     rhs=x_pick[g][:].bitcast(FP8X4),
-                    rhs_scale=x_sc[g],
+                    rhs_scale=placed[:, (TERMS + g) * N : (TERMS + g + 1) * N],
                     start=(g == 0),
-                    stop=(g == 2),
+                    stop=(g == TERMS - 1),
                 )
 
-        pa, pb, inv, rb, ub, roots = {}, {}, {}, {}, {}, {}
+        h, pa, pb, root, inv, rb, ub = {}, {}, {}, {}, {}, {}, {}
 
-        def fetch(t):
-            h = sb("h%d" % t, S, F32)
-            nc.scalar.activation(h[:], h_ps[t][:], ACT.Copy, scale=0.0625)
-            pb[t] = sb("pb%d" % t, W, F32)
-            nc.scalar.activation(pb[t][:], h[:].indirect(n2_t[:]), ACT.Copy)
-            pa[t] = sb("pa%d" % t, W, F32)
-            nc.scalar.activation(pa[t][:], h[:].indirect(n1_t[:]), ACT.Copy)
+        def fetch_pb(t):
+            h[t] = sb("h%d" % t, N, F32)
+            nc.scalar.activation(h[t][:], h_ps[t][:], ACT.Copy, scale=SIXTEENTH)
+            pb[t] = sb("pb%d" % t, PAIRS, F32)
+            nc.scalar.activation(pb[t][:], h[t][:].indirect(n2_t[:]), ACT.Copy)
 
-        def invert(t):
-            size = at("size%d" % t, W, F32, 22528 + 1536) if t == d else sb("size%d" % t, W, F32)
+        def fetch_pa(t):
+            pa[t] = sb("pa%d" % t, PAIRS, F32)
+            nc.scalar.activation(pa[t][:], h[t][:].indirect(n1_t[:]), ACT.Copy)
+
+        def inverse_root(t):
+            size = at("size%d" % t, PAIRS, F32, at_z + size_d_at) if t == D else sb("size%d" % t, PAIRS, F32)
             nc.scalar.activation(size[:], pb[t][:], ACT.Abs)
-            root = sb("root%d" % t, W, F32)
-            nc.scalar.activation(root[:], size[:], ACT.Abs_reciprocal_sqrt, bias=half[:])
-            roots[t] = root
+            root[t] = at("root%d" % t, PAIRS, F32, at_z + root_c_at) if t == C else sb("root%d" % t, PAIRS, F32)
+            nc.scalar.activation(root[t][:], size[:], ACT.Abs_reciprocal_sqrt, bias=half[:])
 
-        def square(t):
-            inv[t] = sb("inv%d" % t, W, F32, tag="ub%d" % a if t == d else None)
-            nc.scalar.activation(inv[t][:], roots[t][:], ACT.Square)
+        def inverse(t):
+            inv[t] = sb("inv%d" % t, PAIRS, F32, after="ub%d" % A if t == D else None)
+            nc.scalar.activation(inv[t][:], root[t][:], ACT.Square)
 
         def larger(t):
-            rb[t] = sb("rb%d" % t, W, F32)
+            rb[t] = sb("rb%d" % t, PAIRS, F32)
             nc.vector.tensor_tensor(rb[t][:], pa[t][:], pb[t][:], ALU.max)
 
         def put_rb(t):
-            ub[t] = sb("ub%d" % t, S, F32)
+            ub[t] = sb("ub%d" % t, N, F32)
             nc.vector.tensor_copy(ub[t][:].indirect(n2_t[:]), rb[t][:])
 
         def put_ra(t):
             nc.vector.tensor_tensor(ub[t][:].indirect(n1_t[:]), pa[t][:], inv[t][:], ALU.mult)
 
-        HALF = S // 2
-        z_bf = []
+        def plane(tile, t):
+            return tile[:].rearrange("p (j t) -> p j t", t=PACK)[:, :, t]
 
-        def z_plane(t, on_vector):
-            for i in range(2):
-                dst = z_bf[i][:].rearrange("p (j t) -> p j t", t=4)[:, :, t]
-                src = ub[t][:, i * HALF : (i + 1) * HALF]
-                if on_vector:
-                    nc.vector.tensor_scalar(dst, src, gs_t[:, t : t + 1], None, ALU.mult)
+        def round_z(t):
+            for i, cols in enumerate(Z_PARTS):
+                if t == D and i < VECTOR_PARTS:
+                    nc.vector.tensor_scalar(plane(z_bf[i], t), ub[t][:, cols], gs_t[:, t : t + 1], None, ALU.mult)
                 else:
-                    nc.scalar.activation(dst, src, ACT.Copy, scale=gs_t[:, t : t + 1])
+                    nc.scalar.activation(plane(z_bf[i], t), ub[t][:, cols], ACT.Copy, scale=gs_t[:, t : t + 1])
 
-        a, b, c, d = ORDER
-        fetch(a)
-        fetch(b)
-        invert(a)
-        square(a)
-        fetch(c)
-        invert(b)
-        square(b)
-        fetch(d)
-        invert(c)
-        invert(d)
-        square(c)
-        z_bf.append(at("z_bf0", 4 * HALF, BF16, 22528))
-        z_bf.append(at("z_bf1", 4 * HALF, BF16, 22528 + 2048))
-        larger(a)
-        put_rb(a)
-        larger(b)
-        put_ra(a)
-        z_plane(a, False)
-        square(d)
-        put_rb(b)
-        larger(c)
-        put_ra(b)
-        larger(d)
-        put_rb(c)
-        put_rb(d)
-        put_ra(c)
-        put_ra(d)
-        for t in ORDER[1:]:
-            z_plane(t, t == d)
+        size_d_at, root_c_at = 512, 2048
+        fetch_pb(A)
+        fetch_pa(A)
+        for t, nxt in ((A, B), (B, C), (C, D)):
+            fetch_pb(nxt)
+            inverse_root(t)
+            fetch_pa(nxt)
+            inverse(t)
+        inverse_root(D)
+        z_bf = [at("z_bf%d" % i, PACK * width(cols), BF16, at_z + 2 * PACK * cols.start) for i, cols in enumerate(Z_PARTS)]
+        larger(A)
+        put_rb(A)
+        for t, nxt in ((A, B), (B, C), (C, D)):
+            larger(nxt)
+            put_ra(t)
+            if t == A:
+                round_z(A)
+                inverse(D)
+            put_rb(nxt)
+        put_ra(D)
+        for t in (B, C, D):
+            round_z(t)
 
-        z_words = sb("z_words", S, U32)
-        z_sc = sb("z_sc", S, U8)
-        for i in range(2):
-            cols = slice(i * HALF, (i + 1) * HALF)
-            nc.vector.quantize_mx(out=z_words[:, cols].bitcast(FP8X4), scales=z_sc[:, cols], in_=z_bf[i][:])
+        z_words = sb("z_words", N, U32)
+        z_scales = sb("z_scales", N, U8)
+        for i, cols in enumerate(Z_PARTS):
+            nc.vector.quantize_mx(out=z_words[:, cols].bitcast(FP8X4), scales=z_scales[:, cols], in_=z_bf[i][:])
 
-        s, s_ps, ds, up, page = {}, {}, {}, {}, {}
+        s, ds, up, page = {}, {}, {}, {}
+        whole = slice(0, N)
 
-        def score(t, pieces, which):
-            if 0 in which:
-                s[t] = sb("s%d" % t, S, F32)
-            width = S // pieces
-            rows = slice(t * P, (t + 1) * P)
-            for i in which:
-                cols = slice(i * width, (i + 1) * width)
-                bank = psum.tile([P, width], F32, name="s_ps%d_%d" % (t, i), tag=("h_ps%d" % t if i == 1 else "s_ps%d" % (c if t == d else t)))
-                s_ps[t] = bank
-                nc.tensor.matmul_mx(
-                    out=bank[:],
-                    lhsT=c_words[:, rows].bitcast(FP8X4),
-                    lhsT_scale=c_sc[:, rows],
-                    rhs=z_words[:, cols].bitcast(FP8X4),
-                    rhs_scale=z_sc[:, cols],
-                    start=True,
-                    stop=True,
-                )
-                nc.scalar.activation(s[t][:, cols], bank[:], ACT.Copy, scale=0.0625)
+        def score(t, cols, bank):
+            acc = psum.tile([P, width(cols)], F32, name="s_ps%d_%d" % (t, cols.start), tag="bank%d" % bank)
+            nc.tensor.matmul_mx(
+                out=acc[:],
+                lhsT=c_words[:, t * P : (t + 1) * P].bitcast(FP8X4),
+                lhsT_scale=c_scales[:, t * P : (t + 1) * P],
+                rhs=z_words[:, cols].bitcast(FP8X4),
+                rhs_scale=z_scales[:, cols],
+                start=True,
+                stop=True,
+            )
+            nc.scalar.activation(s[t][:, cols], acc[:], ACT.Copy, scale=SIXTEENTH)
 
-        def send(t, pieces, which):
-            if 0 in which:
-                ds[t] = sb("ds%d" % t, 2 * S, F32)
-            width = S // pieces
-            for i in which:
-                nc.vector.tensor_copy(
-                    ds[t][:].indirect(n5_t[:, i * width // 16 : (i + 1) * width // 16]), s[t][:, i * width : (i + 1) * width]
-                )
+        def send(t, cols):
+            nc.vector.tensor_copy(ds[t][:].indirect(n5_t[:, cols.start // GROUP : cols.stop // GROUP]), s[t][:, cols])
 
-        def raise_(t):
-            up[t] = sb("up%d" % t, S, F32)
-            if t == c:
-                nc.vector.scalar_tensor_tensor(up[t][:], s_ps[t][:], 0.0625, ds[t][:, 0:S], ALU.mult, ALU.max)
-            else:
-                nc.vector.tensor_tensor(up[t][:], s[t][:], ds[t][:, 0:S], ALU.max)
+        def lift(t):
+            up[t] = sb("up%d" % t, N, F32)
+            nc.vector.tensor_tensor(up[t][:], s[t][:], ds[t][:, whole], ALU.max)
 
         def put_ds(t):
-            page[t] = sb("page%d" % t, U, F32)
-            nc.vector.tensor_copy(page[t][:].indirect(n3_t[:]), ds[t][:, 0:S])
+            page[t] = sb("page%d" % t, SLOTS, F32)
+            nc.vector.tensor_copy(page[t][:].indirect(n3_t[:]), ds[t][:, whole])
 
         def put_up(t):
             nc.vector.tensor_copy(page[t][:].indirect(n4_t[:]), up[t][:])
 
-        Q = U // 4
-        o_bf = [sb("o_bf%d" % i, 4 * Q, BF16) for i in range(4)]
-        rows_out = out_0.rearrange("(p t) w -> p t w", t=4)
+        o_bf = [sb("o_bf%d" % i, PACK * width(cols), BF16) for i, cols in enumerate(O_PARTS)]
+        rows_out = out_0.rearrange("(p t) w -> p t w", t=PACK)
 
-        def hand_out(t, on_vector, chunks=range(4)):
-            if 0 in chunks:
-                nc.sync.dma_start(rows_out[:, t, :], page[t][:])
-            for i in chunks:
-                dst = o_bf[i][:].rearrange("p (j t) -> p j t", t=4)[:, :, t]
-                src = page[t][:, i * Q : (i + 1) * Q]
-                if i < on_vector:
-                    nc.vector.tensor_copy(dst, src)
+        def round_page(t, parts):
+            for i in parts:
+                if t == D and i < VECTOR_PARTS:
+                    nc.vector.tensor_copy(plane(o_bf[i], t), page[t][:, O_PARTS[i]])
                 else:
-                    nc.scalar.copy(dst, src)
+                    nc.scalar.copy(plane(o_bf[i], t), page[t][:, O_PARTS[i]])
 
-        for i in range(2):
-            score(a, 2, [i])
-            score(b, 2, [i])
-        score(c, 1, [0])
-        for i in range(2):
-            send(a, 2, [i])
-            send(b, 2, [i])
-        raise_(a)
-        put_ds(a)
-        send(c, 1, [0])
-        put_up(a)
-        hand_out(a, 0, range(2))
-        raise_(c)
-        score(d, 1, [0])
-        hand_out(a, 0, range(2, 4))
-        put_ds(b)
-        raise_(b)
-        put_ds(c)
-        put_up(b)
-        hand_out(b, 0)
-        send(d, 1, [0])
-        put_up(c)
-        hand_out(c, 0)
-        raise_(d)
-        put_ds(d)
-        put_up(d)
-        hand_out(d, 2)
+        def hand_out(t):
+            put_up(t)
+            nc.sync.dma_start(rows_out[:, t, :], page[t][:])
 
-        o_words = sb("o_words", U, U32)
-        o_sc = sb("o_sc", U, U8)
+        for t in (A, B, C, D):
+            ds[t] = sb("ds%d" % t, 2 * N, F32)
+        for t in (A, B, C):
+            s[t] = sb("s%d" % t, N, F32)
+        for i, cols in enumerate(Z_PARTS):
+            score(A, cols, 2 * i)
+            score(B, cols, 2 * i + 1)
+        score(C, whole, 6)
+        for cols in Z_PARTS:
+            send(A, cols)
+            send(B, cols)
+        lift(A)
+        put_ds(A)
+        send(C, whole)
+        hand_out(A)
+        round_page(A, range(VECTOR_PARTS))
+        s[D] = sb("s%d" % D, N, F32, after="up%d" % A)
+        score(D, whole, 7)
+        round_page(A, range(VECTOR_PARTS, len(O_PARTS)))
+        lift(B)
+        put_ds(B)
+        lift(C)
+        hand_out(B)
+        round_page(B, range(len(O_PARTS)))
+        put_ds(C)
+        send(D, whole)
+        hand_out(C)
+        round_page(C, range(len(O_PARTS)))
+        lift(D)
+        put_ds(D)
+        hand_out(D)
+        round_page(D, range(len(O_PARTS)))
+
+        o_words = sb("o_words", SLOTS, U32)
+        o_scales = sb("o_scales", SLOTS, U8)
         words_out = out_1[0].rearrange("p n t -> p (n t)").bitcast(I32)
-        for i in range(4):
-            cols = slice(i * Q, (i + 1) * Q)
-            nc.vector.quantize_mx(out=o_words[:, cols].bitcast(FP8X4), scales=o_sc[:, cols], in_=o_bf[i][:])
-            if i % 2 == 1:
-                both = slice((i - 1) * Q, (i + 1) * Q)
-                nc.sync.dma_start(words_out[:, both], o_words[:, both].bitcast(I32))
+        for i, cols in enumerate(O_PARTS):
+            nc.vector.quantize_mx(out=o_words[:, cols].bitcast(FP8X4), scales=o_scales[:, cols], in_=o_bf[i][:])
+            if i > 0:
+                done = slice(0 if i == 1 else cols.start, cols.stop)
+                nc.sync.dma_start(words_out[:, done], o_words[:, done].bitcast(I32))
         for q in range(4):
-            queue = nc.scalar if q % 2 else nc.sync
-            queue.dma_start(out_2[0, 4 * q : 4 * q + 4, :].bitcast(I32), o_sc[32 * q : 32 * q + 4, :].bitcast(I32))
+            queue = nc.sync if q % 2 else nc.scalar
+            queue.dma_start(out_2[0, 4 * q : 4 * q + 4, :].bitcast(I32), o_scales[32 * q : 32 * q + 4, :].bitcast(I32))

@@ -57,6 +57,7 @@ def tile_picked_mthhzcratiopagsn_none_po_kernel(
         at_ds_rest = at_ds_first + TERMS * P
         at_d_pick = at_d_tab + 4 * CODEWORDS
         at_z = at_d_pick + 4 * TERMS * N
+        at_o = at_z + 2 * PACK * N
 
         def load_list(name, src):
             tile = pool.tile([P, src.shape[1]], U16, name=name + "_list")
@@ -227,7 +228,7 @@ def tile_picked_mthhzcratiopagsn_none_po_kernel(
         for i, cols in enumerate(Z_PARTS):
             nc.vector.quantize_mx(out=z_words[:, cols].bitcast(FP8X4), scales=z_scales[:, cols], in_=z_bf[i][:])
 
-        s, ds, up, page = {}, {}, {}, {}
+        s, ds, up, page, shares = {}, {}, {}, {}, {}
         whole = slice(0, N)
 
         def score(t, cols, bank):
@@ -246,18 +247,32 @@ def tile_picked_mthhzcratiopagsn_none_po_kernel(
         def send(t, cols):
             nc.vector.tensor_copy(ds[t][:].indirect(n5_t[:, cols.start // GROUP : cols.stop // GROUP]), s[t][:, cols])
 
-        def lift(t):
+        def lift_aside(t):
+            diff = sb("diff%d" % t, N, F32, after={C: "low%d" % A, D: "low%d" % C}.get(t))
+            nc.gpsimd.tensor_tensor(diff[:], s[t][:], ds[t][:, whole], ALU.subtract)
+            sign = sb("sign%d" % t, N, F32)
+            nc.scalar.activation(sign[:], diff[:], ACT.Sign)
+            keep = sb("keep%d" % t, N, F32)
+            nc.scalar.activation(keep[:], sign[:], ACT.Identity, scale=0.5, bias=half[:])
+            drop = sb("drop%d" % t, N, F32)
+            nc.scalar.activation(drop[:], sign[:], ACT.Identity, scale=-0.5, bias=half[:])
+            high = sb("high%d" % t, N, F32)
+            nc.gpsimd.tensor_tensor(high[:], s[t][:], keep[:], ALU.mult)
+            low = sb("low%d" % t, N, F32)
+            nc.gpsimd.tensor_tensor(low[:], ds[t][:, whole], drop[:], ALU.mult)
+            shares[t] = (high, low)
+
+        def join(t):
             up[t] = sb("up%d" % t, N, F32)
-            nc.vector.tensor_tensor(up[t][:], s[t][:], ds[t][:, whole], ALU.max)
+            nc.gpsimd.tensor_tensor(up[t][:], shares[t][0][:], shares[t][1][:], ALU.add)
 
         def put_ds(t):
-            page[t] = sb("page%d" % t, SLOTS, F32)
+            page[t] = sb("page%d" % t, SLOTS, F32, after="page%d" % A if t == D else None)
             nc.vector.tensor_copy(page[t][:].indirect(n3_t[:]), ds[t][:, whole])
 
         def put_up(t):
             nc.vector.tensor_copy(page[t][:].indirect(n4_t[:]), up[t][:])
 
-        o_bf = [sb("o_bf%d" % i, PACK * width(cols), BF16) for i, cols in enumerate(O_PARTS)]
         rows_out = out_0.rearrange("(p t) w -> p t w", t=PACK)
 
         def round_page(t, parts):
@@ -273,33 +288,27 @@ def tile_picked_mthhzcratiopagsn_none_po_kernel(
 
         for t in (A, B, C, D):
             ds[t] = sb("ds%d" % t, 2 * N, F32)
-        for t in (A, B, C):
             s[t] = sb("s%d" % t, N, F32)
         for i, cols in enumerate(Z_PARTS):
             score(A, cols, 2 * i)
             score(B, cols, 2 * i + 1)
         score(C, whole, 6)
+        score(D, whole, 7)
         for cols in Z_PARTS:
             send(A, cols)
             send(B, cols)
-        lift(A)
-        put_ds(A)
         send(C, whole)
-        hand_out(A)
-        round_page(A, range(VECTOR_PARTS))
-        s[D] = sb("s%d" % D, N, F32, after="up%d" % A)
-        score(D, whole, 7)
-        round_page(A, range(VECTOR_PARTS, len(O_PARTS)))
-        lift(B)
-        put_ds(B)
-        lift(C)
-        hand_out(B)
-        round_page(B, range(len(O_PARTS)))
-        put_ds(C)
         send(D, whole)
-        hand_out(C)
-        round_page(C, range(len(O_PARTS)))
-        lift(D)
+        for t in (A, B, C, D):
+            lift_aside(t)
+            join(t)
+        o_all = sb("o_bf", PACK * SLOTS, BF16, after="sign%d" % D)
+        o_bf = [o_all[:, PACK * cols.start : PACK * cols.stop] for cols in O_PARTS]
+        for t in (A, B, C):
+            put_ds(t)
+        for t in (A, B, C):
+            hand_out(t)
+            round_page(t, range(len(O_PARTS)))
         put_ds(D)
         hand_out(D)
         round_page(D, range(len(O_PARTS)))

from contextlib import ExitStack

import concourse.mybir as mybir

F32 = mybir.dt.float32
BF16 = mybir.dt.bfloat16
I32 = mybir.dt.int32
U32 = mybir.dt.uint32
U16 = mybir.dt.uint16
U8 = mybir.dt.uint8
FP8X4 = mybir.dt.float8_e4m3fn_x4
ACT = mybir.ActivationFunctionType
ALU = mybir.AluOpType

P = 128
PACK = 4
GROUP = 16
TOKENS, CODEWORDS = 1024, 2048
N = 512
PAIRS = 256
SLOTS = 1024
TERMS = 3
SIXTEENTH = 0.0625
FLOPS = 4 * 2 * N * N * N

A, B, C, D = 0, 2, 3, 1

Z_PARTS = (slice(0, 128), slice(128, 256), slice(256, 512))
O_PARTS = tuple(slice(256 * i, 256 * (i + 1)) for i in range(4))
VECTOR_PARTS = 2


def width(cols):
    return cols.stop - cols.start


def tile_picked_mthhzcratiopagsn_none_po_kernel(
    tc, x_words, x_scales, d_words, d_scales, gs, offs, k1, hz, k2, hy, k3, n1, n2, cand, n3, n4, n5, out_0, out_1, out_2
):
    nc = tc.nc
    with ExitStack() as ctx:
        pool = ctx.enter_context(tc.tile_pool(name="sb", bufs=1))
        reused = ctx.enter_context(tc.tile_pool(name="reused", bufs=1))
        psum = ctx.enter_context(tc.psum_pool(name="ps", bufs=1))

        def sb(name, cols, dtype, after=None):
            return pool.tile([P, cols], dtype, name=name, tag=after or name, align_bytes=64)

        def at(name, cols, dtype, offset):
            return reused.tile([P, cols], dtype, name=name, align_bytes=64, offset=offset)

        at_d_rest = 0
        at_picked = 4096
        at_d_tab = at_picked + 2 * TERMS * N
        at_x_last = at_d_tab - 1024
        at_ds_first = at_x_last + 4 * N
        at_ds_rest = at_ds_first + TERMS * P
        at_d_pick = at_d_tab + 4 * CODEWORDS
        at_z = at_d_pick + 4 * TERMS * N
        at_o = at_z + 2 * PACK * N

        def load_list(name, src):
            tile = pool.tile([P, src.shape[1]], U16, name=name + "_list")
            nc.sync.dma_start(tile[:], src)
            return tile

        def load_blocks(tile, rows):
            nc.sync.dma_start(tile[:].bitcast(I32), rows.bitcast(I32).unsqueeze(1).to_broadcast([16, 8, rows.shape[1] // 4]))

        def load_words(tile, words):
            nc.sync.dma_start(tile[:].bitcast(I32), words.rearrange("p n t -> p (n t)").bitcast(I32))

        def gather(dst, window, offsets):
            nc.vector.tensor_copy(dst, window[:].indirect(offsets[:]))

        def place(queue, dst, src):
            for c in range(4):
                queue.dma_start(dst[c:P:32, :].bitcast(I32), src[8 * c : P : 32, :].bitcast(I32))

        def dealt(ap):
            return ap.rearrange("p (t m) -> p m t", t=PACK)

        placed = sb("placed", 2 * TERMS * N, U8)
        c_scales = sb("c_scales", N, U8)
        for tile in (placed, c_scales):
            nc.vector.memset(tile[:].bitcast(I32), 0)
        half = sb("half", 1, F32)
        nc.vector.memset(half[:], 0.5)
        warm = sb("warm", 1, F32)
        nc.scalar.activation(warm[:], half[:], ACT.Abs_reciprocal_sqrt, bias=half[:])

        x_blocks = sb("x_blocks", TOKENS, U8)
        load_blocks(x_blocks, x_scales[0])
        hz_t, hy_t, offs_t = load_list("hz", hz), load_list("hy", hy), load_list("offs", offs)
        d_blocks = at("d_blocks", CODEWORDS, U8, at_d_pick)
        load_blocks(d_blocks, d_scales[0])
        k_t = [load_list("k1", k1), load_list("k2", k2), load_list("k3", k3)]
        d_tab = at("d_tab", CODEWORDS, U32, at_d_tab)
        load_words(d_tab, d_words[0])
        x_tab = sb("x_tab", TOKENS, U32)
        load_words(x_tab, x_words[0])
        cand_t, n2_t, n1_t = load_list("cand", cand), load_list("n2", n2), load_list("n1", n1)
        gs_t = sb("gs_cols", PACK, F32)
        nc.sync.dma_start(gs_t[:], gs.rearrange("(p t) o -> p (t o)", t=PACK))
        n5_t, n3_t, n4_t = load_list("n5", n5), load_list("n3", n3), load_list("n4", n4)

        picked = at("picked", 2 * TERMS * N, U8, at_picked)
        for g, offsets in ((4, hz_t), (5, hy_t), (3, offs_t)):
            gather(picked[:, g * N : (g + 1) * N], x_blocks, offsets)
        for g in range(TERMS):
            gather(picked[:, g * N : (g + 1) * N], d_blocks, k_t[g])
        place(nc.scalar, placed, picked)

        d_pick = at("d_pick", TERMS * N, U32, at_d_pick)
        for g in range(TERMS):
            gather(d_pick[:, g * N : (g + 1) * N], d_tab, k_t[g])
        x_pick = [sb("x_offs", N, U32), sb("x_hz", N, U32)]
        gather(x_pick[0][:], x_tab, offs_t)
        gather(x_pick[1][:], x_tab, hz_t)
        d_scale_bytes = placed[:, 0 : TERMS * N]
        d_first = sb("d_first", TERMS * P, U32)
        nc.vector.tensor_copy(d_first[:], d_pick[:].rearrange("p (m t) -> p t m", t=PACK)[:, 0, :])
        ds_first = at("ds_first", TERMS * P, U8, at_ds_first)
        nc.vector.tensor_copy(ds_first[:], d_scale_bytes.rearrange("p (m t) -> p t m", t=PACK)[:, 0, :])
        x_pick.append(at("x_last", N, U32, at_x_last))
        gather(x_pick[2][:], x_tab, hy_t)
        d_rest = at("d_rest", (PACK - 1) * TERMS * P, U32, at_d_rest)
        nc.vector.tensor_copy(
            d_rest[:].rearrange("p (t a b) -> p a t b", t=PACK - 1, b=4),
            d_pick[:].rearrange("p (a b t) -> p a t b", t=PACK, b=4)[:, :, 1:PACK, :],
        )
        ds_rest = at("ds_rest", (PACK - 1) * TERMS * P, U8, at_ds_rest)
        nc.vector.tensor_copy(
            ds_rest[:].rearrange("p (t a b) -> p a t b", t=PACK - 1, b=16),
            d_scale_bytes.rearrange("p (a b t) -> p a t b", t=PACK, b=16)[:, :, 1:PACK, :],
        )

        c_words = at("c_words", N, U32, at_d_pick)
        gather(dealt(c_words[:]), x_tab, cand_t)
        c_picked = at("c_picked", N, U8, at_d_pick + 4 * N)
        gather(dealt(c_picked[:]), x_blocks, cand_t)
        place(nc.sync, c_scales, c_picked)

        h_ps = {}
        for t in (A, B, C, D):
            h_ps[t] = psum.tile([P, N], F32, name="h_ps%d" % t, tag="bank%d" % t)
            words, scales = (d_first, ds_first) if t == 0 else (d_rest, ds_rest)
            for g in range(TERMS):
                first = (TERMS * max(t - 1, 0) + g) * P
                nc.tensor.matmul_mx(
                    out=h_ps[t][:],
                    lhsT=words[:, first : first + P].bitcast(FP8X4),
                    lhsT_scale=scales[:, first : first + P],
                    rhs=x_pick[g][:].bitcast(FP8X4),
                    rhs_scale=placed[:, (TERMS + g) * N : (TERMS + g + 1) * N],
                    start=(g == 0),
                    stop=(g == TERMS - 1),
                )

        h, pa, pb, root, inv, rb, ub = {}, {}, {}, {}, {}, {}, {}

        def fetch_pb(t):
            h[t] = sb("h%d" % t, N, F32)
            nc.scalar.activation(h[t][:], h_ps[t][:], ACT.Copy, scale=SIXTEENTH)
            pb[t] = sb("pb%d" % t, PAIRS, F32)
            nc.scalar.activation(pb[t][:], h[t][:].indirect(n2_t[:]), ACT.Copy)

        def fetch_pa(t):
            pa[t] = sb("pa%d" % t, PAIRS, F32)
            nc.scalar.activation(pa[t][:], h[t][:].indirect(n1_t[:]), ACT.Copy)

        def inverse_root(t):
            size = at("size%d" % t, PAIRS, F32, at_z + size_d_at) if t == D else sb("size%d" % t, PAIRS, F32)
            nc.scalar.activation(size[:], pb[t][:], ACT.Abs)
            root[t] = at("root%d" % t, PAIRS, F32, at_z + root_c_at) if t == C else sb("root%d" % t, PAIRS, F32)
            nc.scalar.activation(root[t][:], size[:], ACT.Abs_reciprocal_sqrt, bias=half[:])

        def inverse(t):
            inv[t] = sb("inv%d" % t, PAIRS, F32, after="ub%d" % A if t == D else None)
            nc.scalar.activation(inv[t][:], root[t][:], ACT.Square)

        def larger(t):
            rb[t] = sb("rb%d" % t, PAIRS, F32)
            nc.vector.tensor_tensor(rb[t][:], pa[t][:], pb[t][:], ALU.max)

        def put_rb(t):
            ub[t] = sb("ub%d" % t, N, F32)
            nc.vector.tensor_copy(ub[t][:].indirect(n2_t[:]), rb[t][:])

        def put_ra(t):
            nc.vector.tensor_tensor(ub[t][:].indirect(n1_t[:]), pa[t][:], inv[t][:], ALU.mult)

        def plane(tile, t):
            return tile[:].rearrange("p (j t) -> p j t", t=PACK)[:, :, t]

        def round_z(t):
            for i, cols in enumerate(Z_PARTS):
                if t == D and i < VECTOR_PARTS:
                    nc.vector.tensor_scalar(plane(z_bf[i], t), ub[t][:, cols], gs_t[:, t : t + 1], None, ALU.mult)
                else:
                    nc.scalar.activation(plane(z_bf[i], t), ub[t][:, cols], ACT.Copy, scale=gs_t[:, t : t + 1])

        size_d_at, root_c_at = 512, 2048
        fetch_pb(A)
        fetch_pa(A)
        for t, nxt in ((A, B), (B, C), (C, D)):
            fetch_pb(nxt)
            inverse_root(t)
            fetch_pa(nxt)
            inverse(t)
        inverse_root(D)
        z_bf = [at("z_bf%d" % i, PACK * width(cols), BF16, at_z + 2 * PACK * cols.start) for i, cols in enumerate(Z_PARTS)]
        larger(A)
        put_rb(A)
        for t, nxt in ((A, B), (B, C), (C, D)):
            larger(nxt)
            put_ra(t)
            if t == A:
                round_z(A)
                inverse(D)
            put_rb(nxt)
        put_ra(D)
        for t in (B, C, D):
            round_z(t)

        z_words = sb("z_words", N, U32)
        z_scales = sb("z_scales", N, U8)
        for i, cols in enumerate(Z_PARTS):
            nc.vector.quantize_mx(out=z_words[:, cols].bitcast(FP8X4), scales=z_scales[:, cols], in_=z_bf[i][:])

        s, ds, up, page, shares = {}, {}, {}, {}, {}
        whole = slice(0, N)

        def score(t, cols, bank):
            acc = psum.tile([P, width(cols)], F32, name="s_ps%d_%d" % (t, cols.start), tag="bank%d" % bank)
            nc.tensor.matmul_mx(
                out=acc[:],
                lhsT=c_words[:, t * P : (t + 1) * P].bitcast(FP8X4),
                lhsT_scale=c_scales[:, t * P : (t + 1) * P],
                rhs=z_words[:, cols].bitcast(FP8X4),
                rhs_scale=z_scales[:, cols],
                start=True,
                stop=True,
            )
            nc.scalar.activation(s[t][:, cols], acc[:], ACT.Copy, scale=SIXTEENTH)

        def send(t, cols):
            nc.vector.tensor_copy(ds[t][:].indirect(n5_t[:, cols.start // GROUP : cols.stop // GROUP]), s[t][:, cols])

        def lift_aside(t):
            diff = sb("diff%d" % t, N, F32, after={C: "low%d" % A, D: "low%d" % C}.get(t))
            nc.gpsimd.tensor_tensor(diff[:], s[t][:], ds[t][:, whole], ALU.subtract)
            sign = sb("sign%d" % t, N, F32)
            nc.scalar.activation(sign[:], diff[:], ACT.Sign)
            keep = sb("keep%d" % t, N, F32)
            nc.scalar.activation(keep[:], sign[:], ACT.Identity, scale=0.5, bias=half[:])
            drop = sb("drop%d" % t, N, F32)
            nc.scalar.activation(drop[:], sign[:], ACT.Identity, scale=-0.5, bias=half[:])
            high = sb("high%d" % t, N, F32)
            nc.gpsimd.tensor_tensor(high[:], s[t][:], keep[:], ALU.mult)
            low = sb("low%d" % t, N, F32)
            nc.gpsimd.tensor_tensor(low[:], ds[t][:, whole], drop[:], ALU.mult)
            shares[t] = (high, low)

        def join(t):
            up[t] = sb("up%d" % t, N, F32)
            nc.gpsimd.tensor_tensor(up[t][:], shares[t][0][:], shares[t][1][:], ALU.add)

        def put_ds(t):
            page[t] = sb("page%d" % t, SLOTS, F32, after="page%d" % A if t == D else None)
            nc.vector.tensor_copy(page[t][:].indirect(n3_t[:]), ds[t][:, whole])

        def put_up(t):
            nc.vector.tensor_copy(page[t][:].indirect(n4_t[:]), up[t][:])

        rows_out = out_0.rearrange("(p t) w -> p t w", t=PACK)

        def round_page(t, parts):
            for i in parts:
                if t == D and i < VECTOR_PARTS:
                    nc.vector.tensor_copy(plane(o_bf[i], t), page[t][:, O_PARTS[i]])
                else:
                    nc.scalar.copy(plane(o_bf[i], t), page[t][:, O_PARTS[i]])

        def hand_out(t):
            put_up(t)
            nc.sync.dma_start(rows_out[:, t, :], page[t][:])

        for t in (A, B, C, D):
            ds[t] = sb("ds%d" % t, 2 * N, F32)
            s[t] = sb("s%d" % t, N, F32)
        for i, cols in enumerate(Z_PARTS):
            score(A, cols, 2 * i)
            score(B, cols, 2 * i + 1)
        score(C, whole, 6)
        score(D, whole, 7)
        for cols in Z_PARTS:
            send(A, cols)
            send(B, cols)
        send(C, whole)
        send(D, whole)
        for t in (A, B, C, D):
            lift_aside(t)
            join(t)
        o_all = sb("o_bf", PACK * SLOTS, BF16, after="sign%d" % D)
        o_bf = [o_all[:, PACK * cols.start : PACK * cols.stop] for cols in O_PARTS]
        for t in (A, B, C):
            put_ds(t)
        for t in (A, B, C):
            hand_out(t)
            round_page(t, range(len(O_PARTS)))
        put_ds(D)
        hand_out(D)
        round_page(D, range(len(O_PARTS)))

        o_words = sb("o_words", SLOTS, U32)
        o_scales = sb("o_scales", SLOTS, U8)
        words_out = out_1[0].rearrange("p n t -> p (n t)").bitcast(I32)
        for i, cols in enumerate(O_PARTS):
            nc.vector.quantize_mx(out=o_words[:, cols].bitcast(FP8X4), scales=o_scales[:, cols], in_=o_bf[i][:])
            if i > 0:
                done = slice(0 if i == 1 else cols.start, cols.stop)
                nc.sync.dma_start(words_out[:, done], o_words[:, done].bitcast(I32))
        for q in range(4):
            queue = nc.sync if q % 2 else nc.scalar
            queue.dma_start(out_2[0, 4 * q : 4 * q + 4, :].bitcast(I32), o_scales[32 * q : 32 * q + 4, :].bitcast(I32))
